import numpy as np
import ml_dtypes


def mxq(x, axis, fmt="e4m3"):
    dtype, down = {"e4m3": (ml_dtypes.float8_e4m3fn, 7), "e5m2": (ml_dtypes.float8_e5m2, 14)}[fmt]
    v = np.moveaxis(np.asarray(x, np.float32).astype(ml_dtypes.bfloat16).astype(np.float64), axis, -1)
    blocks = v.reshape(v.shape[:-1] + (-1, 32))
    amax = np.abs(blocks).max(-1, keepdims=True)
    byte = np.maximum(np.where(amax > 0, np.frexp(amax)[1] - 1 + 127, 0) - down, 1)
    scale = np.exp2(byte - 127.0)
    codes = (blocks / scale).astype(np.float32).astype(dtype).astype(np.float64)
    return np.moveaxis((codes * scale).reshape(v.shape), -1, axis)


WIDE = False


def mx_kscale(k):
    if not WIDE:
        return np.ones(k)
    levels = np.array([10, -10, 5, -5, 0])
    if k % 512:
        return np.exp2(np.random.permutation(np.resize(levels, k // 32))).repeat(32)
    a = np.empty((k // 512, 16))
    for p in range(k // 512):
        a[p, :8] = np.random.permutation(np.resize(levels, 8))
        for g in range(8):
            far = levels[np.abs(levels - a[p, g]) >= 10]
            a[p, g + 8] = far[np.random.randint(len(far))]
    return np.exp2(a.ravel()).repeat(32)


def f64(x):
    return np.asarray(x).astype(np.float64)


def striped(idx):
    return np.tile(idx.reshape(-1, 16).T, (8, 1)).astype(np.uint16)


def unstriped(offs):
    return offs[:16].T.reshape(-1).astype(np.int64)


def pack_weight(w):
    k, n = w.shape
    w = f64(np.asarray(w, np.float32).astype(ml_dtypes.bfloat16)).reshape(k // 32, 32, n)
    amax = np.abs(w).max(1)
    byte = np.clip(np.where(amax > 0, np.frexp(amax)[1] - 1 + 127 - 7, 1), 1, 254)
    scaled = (w * np.exp2(127.0 - byte)[:, None, :]).reshape(k, n).astype(np.float32)
    words = np.ascontiguousarray(scaled.reshape(k // 512, 128, 4, n).transpose(0, 1, 3, 2)).astype(ml_dtypes.float8_e4m3fn).view(np.uint8)
    return words, np.ascontiguousarray(byte.astype(np.uint8).reshape(k // 512, 16, n))


def unpack_weight(words, scales):
    g, p, n, _ = words.shape
    vals = np.ascontiguousarray(words).view(ml_dtypes.float8_e4m3fn).astype(np.float64) * np.repeat(np.exp2(scales.astype(np.float64) - 127.0), 8, axis=1)[..., None]
    return vals.transpose(0, 1, 3, 2).reshape(g * 512, n)


def sigmoid(v):
    return 1.0 / (1.0 + np.exp(-np.maximum(v, -700.0)))


K, T, S, N, H = 1024, 2048, 512, 128, 512


def setup_inputs():
    n = np.random.standard_normal
    s = mx_kscale(K)[:, None]
    u = mx_kscale(H)
    packed_xT = pack_weight(n((K, T)) * s)
    return {
        "x_words": packed_xT[0],
        "x_scales": packed_xT[1],
        "w1": (n((K, H)) / np.sqrt(K) / s).astype(np.float32),
        "w2": (n((K, H)) / np.sqrt(K) / s).astype(np.float32),
        "unit": (np.random.uniform(0.6, 1.4, (H, 1)) * u[:, None]).astype(np.float32),
        "w3": (n((H, N)) / np.sqrt(H) / u[:, None]).astype(np.float32),
        "offs": striped(np.random.permutation(T)[:S]),
        "e1": striped(np.random.permutation(S)),
        "e2": striped(np.random.permutation(S)),
        "fc": striped(np.random.permutation(S)),
    }


def reference(x_words, x_scales, w1, w2, unit, w3, offs, e1, e2, fc):
    xq = unpack_weight(x_words, x_scales)[:, unstriped(offs)]
    ft = mxq(f64(w1), 0, "e4m3").T @ xq
    fa = ft[:, unstriped(e1)]
    sd = mxq(f64(w2), 0, "e4m3").T @ xq
    sa = sd[:, unstriped(e1)]
    s1 = np.tanh(sa)
    sb = sd[:, unstriped(e2)]
    s2 = np.tanh(sb)
    tt = (np.abs(s1) + 0.1) / (np.abs(s1) + np.abs(s2) + 0.2)
    fb = ft[:, unstriped(e2)]
    vert = fa * (-1.0 * tt + 1.0) + fb * tt
    cross = sigmoid(-4.0 * (s1 * s2))
    vc = vert * cross
    vf = vc[:, unstriped(fc)]
    hid = f64(unit) * vf
    return mxq(f64(w3), 0, "e4m3").T @ mxq(hid, 0, "e4m3")

@@ -1,0 +1,220 @@
+from contextlib import ExitStack
+
+import concourse.mybir as mybir
+from concourse.masks import make_identity
+
+K, T, S, N, H = 1024, 2048, 512, 128, 512
+FLOPS = 2 * (2 * K * H * S + H * N * S)
+
+F32 = mybir.dt.float32
+BF16 = mybir.dt.bfloat16
+I32 = mybir.dt.int32
+U32 = mybir.dt.uint32
+U16 = mybir.dt.uint16
+U8 = mybir.dt.uint8
+FP8X4 = mybir.dt.float8_e4m3fn_x4
+ACT = mybir.ActivationFunctionType
+ALU = mybir.AluOpType
+
+P = 128
+PACK = 4
+PASSES = K // (P * PACK)
+TILES = H // P
+CHUNKS = S // P
+HALF = S // 2
+SIGNED_WINDOW = 704
+FEATURE_WINDOW = 528
+
+
+def tile_picked_ymarch_vert_p_kernel(tc, x_words, x_scales, w1, w2, unit, w3, offs, e1, e2, fc, out):
+    nc = tc.nc
+    with ExitStack() as ctx:
+        held = ctx.enter_context(tc.tile_pool(name="held", bufs=1))
+        ring = ctx.enter_context(tc.tile_pool(name="ring", bufs=2))
+        psum = ctx.enter_context(tc.psum_pool(name="psum", bufs=1))
+
+        def load_list(name, dram):
+            tile = held.tile([P, S // 16], U16, name=name)
+            nc.sync.dma_start(tile[:], dram)
+            return tile
+
+        def load_words(o):
+            tile = held.tile([P, T], U32, name="x_words_%d" % o)
+            nc.sync.dma_start(tile[:].bitcast(I32), x_words[o].rearrange("p n j -> p (n j)").bitcast(I32))
+            return tile
+
+        def load_weight(name, w, t):
+            raw = held.tile([P, PASSES, PACK, P], F32, name="%s_raw_%d" % (name, t))
+            for o in range(PASSES):
+                rows = w[o * P * PACK : (o + 1) * P * PACK, t * P : (t + 1) * P]
+                nc.sync.dma_start(raw[:, o], rows.rearrange("(p j) m -> p j m", j=PACK))
+            return raw
+
+        offs_sb = load_list("offs_sb", offs)
+        xw = [load_words(0)]
+        xs = held.tile([P, T], U8, name="x_scale_rows")
+        nc.vector.memset(xs[:].bitcast(I32), 0)
+        for q in range(4):
+            nc.sync.dma_start(xs[32 * q : 32 * q + 4 * PASSES, :].bitcast(I32), x_scales[:, 4 * q : 4 * q + 4, :].bitcast(I32))
+        w2_raw = [load_weight("w2", w2, 0)]
+        xw.append(load_words(1))
+        w2_raw.append(load_weight("w2", w2, 1))
+        e1_sb = load_list("e1_sb", e1)
+        e2_sb = load_list("e2_sb", e2)
+        w2_raw.extend([load_weight("w2", w2, t) for t in range(2, TILES)])
+        unit_sb = held.tile([P, TILES], F32, name="unit_sb")
+        with nc.allow_non_contiguous_dma(reason="one value of unit a partition and feature tile"):
+            nc.sync.dma_start(unit_sb[:], unit.rearrange("(t p) o -> p (t o)", p=P))
+        w1_raw = [load_weight("w1", w1, t) for t in range(TILES)]
+        w3_raw = held.tile([P, PACK, N], F32, name="w3_raw")
+        nc.sync.dma_start(w3_raw[:], w3.rearrange("(p j) m -> p j m", j=PACK))
+        fc_sb = load_list("fc_sb", fc)
+
+        ident = held.tile([P, P], F32, name="ident")
+        make_identity(nc, ident[:])
+        signed = [held.tile([P, SIGNED_WINDOW], F32, name="signed_%d" % t) for t in range(TILES)]
+        feat = [held.tile([P, FEATURE_WINDOW], F32, name="feat_%d" % t) for t in range(TILES)]
+        for tile in signed + feat:
+            nc.gpsimd.memset(tile[:, S:], 0.0)
+
+        xg_scales = held.tile([P, S], U8, name="xg_scales", align_bytes=64)
+        xg = [held.tile([P, S], U32, name="xg_words_%d" % o, align_bytes=64) for o in range(PASSES)]
+        nc.vector.tensor_copy(xg[0][:], xw[0][:].indirect(offs_sb[:]))
+        nc.vector.tensor_copy(xg_scales[:], xs[:].indirect(offs_sb[:]))
+
+        def quantise_weight(name, raw, on_scalar):
+            grouped = ring.tile([P, PASSES * P * PACK], BF16, name="grouped", align_bytes=64, bufs=3)
+            dst = grouped[:].rearrange("p (o c i j) -> p o c j i", o=PASSES, i=4, j=PACK)
+            src = raw[:].rearrange("p o j (c i) -> p o c j i", i=4)
+            if on_scalar:
+                nc.scalar.copy(dst, src)
+            else:
+                nc.vector.tensor_copy(dst, src)
+            codes = held.tile([P, PASSES * P], U32, name=name + "_codes", align_bytes=64)
+            scales = held.tile([P, PASSES * P], U8, name=name + "_scales", align_bytes=64)
+            nc.vector.quantize_mx(out=codes[:].bitcast(FP8X4), scales=scales[:], in_=grouped[:])
+            return codes, scales
+
+        def product(weight):
+            codes, scales = weight
+            acc = psum.tile([P, S], F32, name="acc", bufs=2)
+            for o in range(PASSES):
+                cols = slice(o * P, (o + 1) * P)
+                nc.tensor.matmul_mx(
+                    out=acc[:],
+                    lhsT=codes[:, cols].bitcast(FP8X4),
+                    lhsT_scale=scales[:, cols],
+                    rhs=xg[o][:].bitcast(FP8X4),
+                    rhs_scale=xg_scales[4 * o :, :],
+                    start=(o == 0),
+                    stop=(o == PASSES - 1),
+                )
+            return acc
+
+        def turned_sum(tag, bufs, terms):
+            bank = psum.tile([P, S], F32, name=tag, bufs=bufs)
+            for c in range(CHUNKS):
+                cols = slice(c * P, (c + 1) * P)
+                for i, term in enumerate(terms):
+                    nc.tensor.matmul(
+                        bank[:, cols], term[:, cols], ident[:], start=(i == 0), stop=(i == len(terms) - 1), is_transpose=True
+                    )
+            return bank
+
+        w2q = [quantise_weight("w2_0", w2_raw[0], True)]
+        nc.vector.tensor_copy(xg[1][:], xw[1][:].indirect(offs_sb[:]))
+        w2q.append(quantise_weight("w2_1", w2_raw[1], True))
+
+        ends = [held.tile([P, 2, S], F32, name="ends_%d" % t) for t in range(TILES)]
+        mags = [held.tile([P, 2, S], F32, name="mags_%d" % t) for t in range(TILES)]
+        tanh2p = [held.tile([P, S], F32, name="tanh2p_%d" % t) for t in range(TILES)]
+        w1q = []
+        for t in range(TILES):
+            nc.scalar.activation(signed[t][:, :S], product(w2q[t])[:], ACT.Tanh)
+            nc.scalar.activation(ends[t][:, 0, :], signed[t][:].indirect(e1_sb[:]), ACT.Copy)
+            nc.vector.tensor_copy(ends[t][:, 1, :], signed[t][:].indirect(e2_sb[:]))
+            if t + 2 < TILES:
+                w2q.append(quantise_weight("w2_%d" % (t + 2), w2_raw[t + 2], False))
+            else:
+                w1q.append(quantise_weight("w1_%d" % (t - 2), w1_raw[t - 2], False))
+            prod = ring.tile([P, S], F32, name="prod")
+            nc.vector.tensor_tensor(prod[:], ends[t][:, 0, :], ends[t][:, 1, :], ALU.mult)
+            nc.scalar.activation(mags[t][:], ends[t][:], ACT.Abs)
+            turned = turned_sum("turn_%d" % (t % 2), 1, [prod])
+            nc.scalar.activation(tanh2p[t][:], turned[:], ACT.Tanh, scale=2.0)
+
+        w1q.extend([quantise_weight("w1_%d" % t, w1_raw[t], False) for t in range(2, TILES)])
+        gain = held.tile([P, TILES], F32, name="gain")
+        nc.vector.tensor_scalar(gain[:], unit_sb[:], -0.5, None, ALU.mult)
+        w3_grouped = held.tile([P, N * PACK], BF16, name="w3_grouped", align_bytes=64)
+        nc.vector.tensor_copy(
+            w3_grouped[:].rearrange("p (c i j) -> p c j i", i=4, j=PACK), w3_raw[:].rearrange("p j (c i) -> p c j i", i=4)
+        )
+        w3_codes = held.tile([P, N], U32, name="w3_codes", align_bytes=64)
+        w3_scales = held.tile([P, N], U8, name="w3_scales", align_bytes=64)
+        nc.vector.quantize_mx(out=w3_codes[:].bitcast(FP8X4), scales=w3_scales[:], in_=w3_grouped[:])
+
+        hid_t = [held.tile([P, 2, H], BF16, name="hid_t_%d" % h) for h in range(2)]
+        for t in range(TILES):
+            nc.scalar.activation(feat[t][:, :S], product(w1q[t])[:], ACT.Copy, scale=gain[:, t : t + 1])
+            a2 = ring.tile([P, S], F32, name="a2")
+            nc.vector.tensor_scalar(a2[:], mags[t][:, 1, :], 0.1, None, ALU.add)
+            den = turned_sum("turn_1", 1, [mags[t][:, 0, :], a2])
+            fb = ring.tile([P, S], F32, name="fb")
+            nc.scalar.activation(fb[:], feat[t][:].indirect(e2_sb[:]), ACT.Copy)
+            n1 = ring.tile([P, S], F32, name="n1")
+            nc.vector.tensor_tensor(n1[:], feat[t][:].indirect(e1_sb[:]), a2[:], ALU.mult)
+            den2 = ring.tile([P, S], F32, name="den2")
+            nc.scalar.activation(den2[:], den[:], ACT.Square, bias=0.1)
+            rden = ring.tile([P, S], F32, name="rden")
+            nc.scalar.activation(rden[:], den2[:], ACT.Abs_reciprocal_sqrt)
+            n2 = ring.tile([P, S], F32, name="n2")
+            nc.vector.scalar_tensor_tensor(n2[:], mags[t][:, 0, :], 0.1, fb[:], ALU.add, ALU.mult)
+            num = turned_sum("num", 2, [n1, n2])
+            factor = ring.tile([P, S], F32, name="factor")
+            nc.vector.scalar_tensor_tensor(factor[:], tanh2p[t][:], -1.0, rden[:], ALU.add, ALU.mult)
+            for h in range(2):
+                cols = slice(h * HALF, (h + 1) * HALF)
+                nc.vector.tensor_tensor(
+                    hid_t[h][:, :, t * P : (t + 1) * P],
+                    num[:, cols].rearrange("p (c f) -> p c f", c=2),
+                    factor[:, cols].rearrange("p (c f) -> p c f", c=2),
+                    ALU.mult,
+                )
+
+        shaded = held.tile([P, S], F32, name="shaded")
+        for h in range(2):
+            words = hid_t[h][:].rearrange("p c f -> p (c f)").bitcast(F32)
+            back = psum.tile([P, 2, 2, P], F32, name="back", bufs=2)
+            for c in range(2):
+                for u in range(2):
+                    nc.tensor.transpose(back[:, c, u, :], words[:, 2 * P * c + u : 2 * P * (c + 1) : 2], ident[:])
+            hid = ring.tile([P, HALF * PACK], BF16, name="hid", align_bytes=64)
+            dst = hid[:].bitcast(F32).rearrange("p (c e u) -> p c e u", c=2, u=2)
+            src = back[:].rearrange("p c u e -> p c e u")
+            if h == 0:
+                nc.scalar.copy(dst, src)
+            else:
+                nc.vector.tensor_copy(dst, src)
+            hid_codes = ring.tile([P, HALF], U32, name="hid_codes", align_bytes=64)
+            hid_scales = ring.tile([P, HALF], U8, name="hid_scales", align_bytes=64)
+            nc.vector.quantize_mx(out=hid_codes[:].bitcast(FP8X4), scales=hid_scales[:], in_=hid[:])
+            acc = psum.tile([P, S], F32, name="acc", bufs=2)
+            nc.tensor.matmul_mx(
+                out=acc[:, :HALF],
+                lhsT=w3_codes[:].bitcast(FP8X4),
+                lhsT_scale=w3_scales[:],
+                rhs=hid_codes[:].bitcast(FP8X4),
+                rhs_scale=hid_scales[:],
+                start=True,
+                stop=True,
+            )
+            nc.scalar.copy(shaded[:, h * HALF : (h + 1) * HALF], acc[:, :HALF])
+        for h in range(2):
+            faces = held.tile([P, HALF], F32, name="faces_%d" % h)
+            picked = shaded[:].indirect(fc_sb[:, h * HALF // 16 : (h + 1) * HALF // 16])
+            if h == 0:
+                nc.vector.tensor_copy(faces[:], picked)
+            else:
+                nc.scalar.activation(faces[:], picked, ACT.Copy)
+            nc.sync.dma_start(out[:, h * HALF : (h + 1) * HALF], faces[:])

@@ -20,10 +20,11 @@ P = 128
 PACK = 4
 PASSES = K // (P * PACK)
 TILES = H // P
-CHUNKS = S // P
 HALF = S // 2
-SIGNED_WINDOW = 704
-FEATURE_WINDOW = 528
+PARTS = 4
+PART = S // PARTS
+SPLIT = 2
+WINDOW = 704
 
 
 def tile_picked_ymarch_vert_p_kernel(tc, x_words, x_scales, w1, w2, unit, w3, offs, e1, e2, fc, out):
@@ -39,65 +40,69 @@ def tile_picked_ymarch_vert_p_kernel(tc, x_words, x_scales, w1, w2, unit, w3, of
             return tile
 
         def load_words(o):
-            tile = held.tile([P, T], U32, name="x_words_%d" % o)
+            tile = held.tile([P, T], U32, name="x_words_%d" % o, tag="x_words_%d" % o, align_bytes=64)
             nc.sync.dma_start(tile[:].bitcast(I32), x_words[o].rearrange("p n j -> p (n j)").bitcast(I32))
             return tile
 
-        def load_weight(name, w, t):
-            raw = held.tile([P, PASSES, PACK, P], F32, name="%s_raw_%d" % (name, t))
+        def load_weight(name, w, t0, count):
+            raw = held.tile([P, PASSES, PACK, count * P], F32, name="%s_raw_%d" % (name, t0))
             for o in range(PASSES):
-                rows = w[o * P * PACK : (o + 1) * P * PACK, t * P : (t + 1) * P]
+                rows = w[o * P * PACK : (o + 1) * P * PACK, t0 * P : (t0 + count) * P]
                 nc.sync.dma_start(raw[:, o], rows.rearrange("(p j) m -> p j m", j=PACK))
-            return raw
+            return [raw[:, :, :, i * P : (i + 1) * P] for i in range(count)]
 
-        offs_sb = load_list("offs_sb", offs)
-        xw = [load_words(0)]
-        xs = held.tile([P, T], U8, name="x_scale_rows")
-        nc.vector.memset(xs[:].bitcast(I32), 0)
+        xs = held.tile([P, T], U8, name="x_scale_rows", tag="scale_rows_then_words", align_bytes=64)
+        nc.gpsimd.memset(xs[:].bitcast(I32), 0)
         for q in range(4):
-            nc.sync.dma_start(xs[32 * q : 32 * q + 4 * PASSES, :].bitcast(I32), x_scales[:, 4 * q : 4 * q + 4, :].bitcast(I32))
-        w2_raw = [load_weight("w2", w2, 0)]
-        xw.append(load_words(1))
-        w2_raw.append(load_weight("w2", w2, 1))
-        e1_sb = load_list("e1_sb", e1)
-        e2_sb = load_list("e2_sb", e2)
-        w2_raw.extend([load_weight("w2", w2, t) for t in range(2, TILES)])
+            nc.gpsimd.dma_start(xs[32 * q : 32 * q + 4 * PASSES, :].bitcast(I32), x_scales[:, 4 * q : 4 * q + 4, :].bitcast(I32))
+        first_raw = [held.tile([P, PACK, P], F32, name="w2_first_%d" % o) for o in range(PASSES)]
+
+        def load_first(o):
+            nc.sync.dma_start(first_raw[o][:], w2[o * P * PACK : (o + 1) * P * PACK, :P].rearrange("(p j) m -> p j m", j=PACK))
+
+        for o in range(PASSES):
+            load_first(o)
+        offs_sb = load_list("offs_sb", offs)
+        xw = [load_words(o) for o in range(PASSES)]
+        raws = [None]
+        lists = (load_list("e1_sb", e1), load_list("e2_sb", e2))
+        raws.extend(load_weight("w2", w2, 1, 1))
+        raws.extend(load_weight("w2", w2, 2, 1))
+        raws.extend(load_weight("w2", w2, 3, 1))
         unit_sb = held.tile([P, TILES], F32, name="unit_sb")
         with nc.allow_non_contiguous_dma(reason="one value of unit a partition and feature tile"):
             nc.sync.dma_start(unit_sb[:], unit.rearrange("(t p) o -> p (t o)", p=P))
-        w1_raw = [load_weight("w1", w1, t) for t in range(TILES)]
+        raws.extend(load_weight("w1", w1, 0, 2))
+        raws.extend(load_weight("w1", w1, 2, 2))
         w3_raw = held.tile([P, PACK, N], F32, name="w3_raw")
         nc.sync.dma_start(w3_raw[:], w3.rearrange("(p j) m -> p j m", j=PACK))
         fc_sb = load_list("fc_sb", fc)
 
         ident = held.tile([P, P], F32, name="ident")
         make_identity(nc, ident[:])
-        signed = [held.tile([P, SIGNED_WINDOW], F32, name="signed_%d" % t) for t in range(TILES)]
-        feat = [held.tile([P, FEATURE_WINDOW], F32, name="feat_%d" % t) for t in range(TILES)]
+        signed = [held.tile([P, WINDOW], F32, name="signed_%d" % t, tag="signed_%d" % t, align_bytes=64) for t in range(TILES)]
+        feat = [held.tile([P, WINDOW], F32, name="feat_%d" % t) for t in range(TILES)]
         for tile in signed + feat:
             nc.gpsimd.memset(tile[:, S:], 0.0)
 
-        xg_scales = held.tile([P, S], U8, name="xg_scales", align_bytes=64)
-        xg = [held.tile([P, S], U32, name="xg_words_%d" % o, align_bytes=64) for o in range(PASSES)]
-        nc.vector.tensor_copy(xg[0][:], xw[0][:].indirect(offs_sb[:]))
-        nc.vector.tensor_copy(xg_scales[:], xs[:].indirect(offs_sb[:]))
-
-        def quantise_weight(name, raw, on_scalar):
-            grouped = ring.tile([P, PASSES * P * PACK], BF16, name="grouped", align_bytes=64, bufs=3)
+        def quantise_weight(i, grouped, on_scalar=False):
             dst = grouped[:].rearrange("p (o c i j) -> p o c j i", o=PASSES, i=4, j=PACK)
-            src = raw[:].rearrange("p o j (c i) -> p o c j i", i=4)
+            src = raws[i].rearrange("p o j (c i) -> p o c j i", i=4)
             if on_scalar:
                 nc.scalar.copy(dst, src)
             else:
                 nc.vector.tensor_copy(dst, src)
-            codes = held.tile([P, PASSES * P], U32, name=name + "_codes", align_bytes=64)
-            scales = held.tile([P, PASSES * P], U8, name=name + "_scales", align_bytes=64)
+            codes = held.tile([P, PASSES * P], U32, name="w_codes_%d" % i, align_bytes=64)
+            scales = held.tile([P, PASSES * P], U8, name="w_scales_%d" % i, align_bytes=64)
             nc.vector.quantize_mx(out=codes[:].bitcast(FP8X4), scales=scales[:], in_=grouped[:])
             return codes, scales
 
+        def grouped_tile(i, tag):
+            return held.tile([P, PASSES * P * PACK], BF16, name="grouped_%d" % i, tag=tag, align_bytes=64)
+
         def product(weight):
             codes, scales = weight
-            acc = psum.tile([P, S], F32, name="acc", bufs=2)
+            acc = psum.tile([P, S], F32, name="shade", bufs=2)
             for o in range(PASSES):
                 cols = slice(o * P, (o + 1) * P)
                 nc.tensor.matmul_mx(
@@ -111,9 +116,9 @@ def tile_picked_ymarch_vert_p_kernel(tc, x_words, x_scales, w1, w2, unit, w3, of
                 )
             return acc
 
-        def turned_sum(tag, bufs, terms):
+        def turned_sum(tag, bufs, terms, width=S):
             bank = psum.tile([P, S], F32, name=tag, bufs=bufs)
-            for c in range(CHUNKS):
+            for c in range(width // P):
                 cols = slice(c * P, (c + 1) * P)
                 for i, term in enumerate(terms):
                     nc.tensor.matmul(
@@ -121,87 +126,124 @@ def tile_picked_ymarch_vert_p_kernel(tc, x_words, x_scales, w1, w2, unit, w3, of
                     )
             return bank
 
-        w2q = [quantise_weight("w2_0", w2_raw[0], True)]
+        def gather(dst, window, offsets, on_vector):
+            if on_vector:
+                nc.vector.tensor_copy(dst, window[:].indirect(offsets))
+            else:
+                nc.scalar.activation(dst, window[:].indirect(offsets), ACT.Copy)
+
+        first_codes = held.tile([P, PASSES * P], U32, name="first_codes", align_bytes=64)
+        first_scales = held.tile([P, PASSES * P], U8, name="first_scales", align_bytes=64)
+
+        def quantise_first(o):
+            grouped = held.tile([P, P * PACK], BF16, name="first_grouped_%d" % o, align_bytes=64)
+            nc.scalar.copy(grouped[:].rearrange("p (c i j) -> p c j i", i=4, j=PACK), first_raw[o][:].rearrange("p j (c i) -> p c j i", i=4))
+            cols = slice(o * P, (o + 1) * P)
+            nc.vector.quantize_mx(out=first_codes[:, cols].bitcast(FP8X4), scales=first_scales[:, cols], in_=grouped[:])
+
+        for o in range(PASSES):
+            quantise_first(o)
+        wq = [(first_codes, first_scales)]
+        xg_scales = held.tile([P, S], U8, name="xg_scales", align_bytes=64)
+        xg = [held.tile([P, S], U32, name="xg_words_0", align_bytes=64)]
+        nc.vector.tensor_copy(xg[0][:], xw[0][:].indirect(offs_sb[:]))
+        nc.vector.tensor_copy(xg_scales[:], xs[:].indirect(offs_sb[:]))
+        xg.append(held.tile([P, S], U32, name="xg_words_1", tag="scale_rows_then_words", align_bytes=64))
         nc.vector.tensor_copy(xg[1][:], xw[1][:].indirect(offs_sb[:]))
-        w2q.append(quantise_weight("w2_1", w2_raw[1], True))
+        wq.append(quantise_weight(1, grouped_tile(1, "x_words_1")))
+
+        w3_codes = held.tile([P, N], U32, name="w3_codes", align_bytes=64)
+        w3_scales = held.tile([P, N], U8, name="w3_scales", align_bytes=64)
+
+        def quantise_w3():
+            w3_grouped = held.tile([P, N * PACK], BF16, name="w3_grouped", tag="signed_3", align_bytes=64)
+            nc.vector.tensor_copy(
+                w3_grouped[:].rearrange("p (c i j) -> p c j i", i=4, j=PACK), w3_raw[:].rearrange("p j (c i) -> p c j i", i=4)
+            )
+            nc.vector.quantize_mx(out=w3_codes[:].bitcast(FP8X4), scales=w3_scales[:], in_=w3_grouped[:])
 
         ends = [held.tile([P, 2, S], F32, name="ends_%d" % t) for t in range(TILES)]
         mags = [held.tile([P, 2, S], F32, name="mags_%d" % t) for t in range(TILES)]
         tanh2p = [held.tile([P, S], F32, name="tanh2p_%d" % t) for t in range(TILES)]
-        w1q = []
-        for t in range(TILES):
-            nc.scalar.activation(signed[t][:, :S], product(w2q[t])[:], ACT.Tanh)
-            nc.scalar.activation(ends[t][:, 0, :], signed[t][:].indirect(e1_sb[:]), ACT.Copy)
-            nc.vector.tensor_copy(ends[t][:, 1, :], signed[t][:].indirect(e2_sb[:]))
-            if t + 2 < TILES:
-                w2q.append(quantise_weight("w2_%d" % (t + 2), w2_raw[t + 2], False))
-            else:
-                w1q.append(quantise_weight("w1_%d" % (t - 2), w1_raw[t - 2], False))
-            prod = ring.tile([P, S], F32, name="prod")
-            nc.vector.tensor_tensor(prod[:], ends[t][:, 0, :], ends[t][:, 1, :], ALU.mult)
+        factor = [held.tile([P, S], F32, name="factor_%d" % t) for t in range(TILES)]
+
+        den2 = [held.tile([P, S], F32, name="den2_%d" % t) for t in range(TILES)]
+
+        def squared(t):
+            den = turned_sum("turn_%d" % (t % 2), 1, [mags[t][:, 0, :], mags[t][:, 1, :]])
+            nc.scalar.activation(den2[t][:], den[:], ACT.Square, scale=2.0, bias=0.4)
+
+        def magnitudes(t):
             nc.scalar.activation(mags[t][:], ends[t][:], ACT.Abs)
-            turned = turned_sum("turn_%d" % (t % 2), 1, [prod])
-            nc.scalar.activation(tanh2p[t][:], turned[:], ACT.Tanh, scale=2.0)
 
-        w1q.extend([quantise_weight("w1_%d" % t, w1_raw[t], False) for t in range(2, TILES)])
-        gain = held.tile([P, TILES], F32, name="gain")
-        nc.vector.tensor_scalar(gain[:], unit_sb[:], -0.5, None, ALU.mult)
-        w3_grouped = held.tile([P, N * PACK], BF16, name="w3_grouped", align_bytes=64)
-        nc.vector.tensor_copy(
-            w3_grouped[:].rearrange("p (c i j) -> p c j i", i=4, j=PACK), w3_raw[:].rearrange("p j (c i) -> p c j i", i=4)
-        )
-        w3_codes = held.tile([P, N], U32, name="w3_codes", align_bytes=64)
-        w3_scales = held.tile([P, N], U8, name="w3_scales", align_bytes=64)
-        nc.vector.quantize_mx(out=w3_codes[:].bitcast(FP8X4), scales=w3_scales[:], in_=w3_grouped[:])
-
-        hid_t = [held.tile([P, 2, H], BF16, name="hid_t_%d" % h) for h in range(2)]
         for t in range(TILES):
-            nc.scalar.activation(feat[t][:, :S], product(w1q[t])[:], ACT.Copy, scale=gain[:, t : t + 1])
-            a2 = ring.tile([P, S], F32, name="a2")
-            nc.vector.tensor_scalar(a2[:], mags[t][:, 1, :], 0.1, None, ALU.add)
-            den = turned_sum("turn_1", 1, [mags[t][:, 0, :], a2])
-            fb = ring.tile([P, S], F32, name="fb")
-            nc.scalar.activation(fb[:], feat[t][:].indirect(e2_sb[:]), ACT.Copy)
-            n1 = ring.tile([P, S], F32, name="n1")
-            nc.vector.tensor_tensor(n1[:], feat[t][:].indirect(e1_sb[:]), a2[:], ALU.mult)
-            den2 = ring.tile([P, S], F32, name="den2")
-            nc.scalar.activation(den2[:], den[:], ACT.Square, bias=0.1)
-            rden = ring.tile([P, S], F32, name="rden")
-            nc.scalar.activation(rden[:], den2[:], ACT.Abs_reciprocal_sqrt)
-            n2 = ring.tile([P, S], F32, name="n2")
-            nc.vector.scalar_tensor_tensor(n2[:], mags[t][:, 0, :], 0.1, fb[:], ALU.add, ALU.mult)
-            num = turned_sum("num", 2, [n1, n2])
-            factor = ring.tile([P, S], F32, name="factor")
-            nc.vector.scalar_tensor_tensor(factor[:], tanh2p[t][:], -1.0, rden[:], ALU.add, ALU.mult)
-            for h in range(2):
-                cols = slice(h * HALF, (h + 1) * HALF)
+            nc.scalar.activation(signed[t][:, :S], product(wq[t])[:], ACT.Tanh)
+            for k in range(2):
+                gather(ends[t][:, k, :], signed[t], lists[k][:], k == 1)
+            prod = ring.tile([P, S], F32, name="prod", tag="prod_%d" % (t % 2), bufs=1)
+            nc.vector.tensor_tensor(prod[:], ends[t][:, 0, :], ends[t][:, 1, :], ALU.mult)
+            turned = turned_sum("turn_%d" % (t % 2), 1, [prod])
+            if t < TILES - 1:
+                wq.extend([quantise_weight(i, grouped_tile(i, "signed_%d" % t)) for i in (2 * t + 2, 2 * t + 3)])
+            else:
+                quantise_w3()
+            if not (t >= 2):
+                magnitudes(t)
+            nc.scalar.activation(tanh2p[t][:], turned[:], ACT.Tanh, scale=-2.0)
+
+        rden = ring.tile([P, TILES, S], F32, name="rden", tag="prod_1", bufs=1)
+
+        def edge_factor(t, lo=0, hi=S):
+            nc.scalar.activation(rden[:, t, lo:hi], den2[t][:, lo:hi], ACT.Abs_reciprocal_sqrt)
+            nc.vector.scalar_tensor_tensor(factor[t][:, lo:hi], tanh2p[t][:, lo:hi], 1.0, rden[:, t, lo:hi], ALU.add, ALU.mult)
+
+        hid_t = [held.tile([P, PART // P, H], BF16, name="hid_t_%d" % h) for h in range(PARTS)]
+
+        def features(t):
+            acc = product(wq[TILES + t])
+            if t < 1:
+                nc.vector.tensor_scalar(feat[t][:, :S], acc[:], unit_sb[:, t : t + 1], None, ALU.mult)
+            else:
+                nc.scalar.activation(feat[t][:, :S], acc[:], ACT.Copy, scale=unit_sb[:, t : t + 1])
+
+        def numerators(t, lo, hi):
+            width = hi - lo
+            terms = []
+            for k in range(2):
+                picked = ring.tile([P, S], F32, name="picked", bufs=4)
+                gather(picked[:, :width], feat[t], lists[k][:, lo // 16 : hi // 16], k == 0)
+                term = ring.tile([P, S], F32, name="term", bufs=4)
+                nc.vector.scalar_tensor_tensor(term[:, :width], mags[t][:, 1 - k, lo:hi], 0.1, picked[:, :width], ALU.add, ALU.mult)
+                terms.append(term)
+            return turned_sum("num", 4, terms, width)
+
+        def hidden(t, num, lo, hi):
+            for h in range(lo // PART, hi // PART):
                 nc.vector.tensor_tensor(
                     hid_t[h][:, :, t * P : (t + 1) * P],
-                    num[:, cols].rearrange("p (c f) -> p c f", c=2),
-                    factor[:, cols].rearrange("p (c f) -> p c f", c=2),
+                    num[:, h * PART - lo : (h + 1) * PART - lo].rearrange("p (c f) -> p c f", f=P),
+                    factor[t][:, h * PART : (h + 1) * PART].rearrange("p (c f) -> p c f", f=P),
                     ALU.mult,
                 )
 
         shaded = held.tile([P, S], F32, name="shaded")
-        for h in range(2):
+
+        def shade(h):
+            chunks = PART // P
             words = hid_t[h][:].rearrange("p c f -> p (c f)").bitcast(F32)
-            back = psum.tile([P, 2, 2, P], F32, name="back", bufs=2)
-            for c in range(2):
+            back = psum.tile([P, chunks, 2, P], F32, name="turn_%d" % (h % 2))
+            for c in range(chunks):
                 for u in range(2):
                     nc.tensor.transpose(back[:, c, u, :], words[:, 2 * P * c + u : 2 * P * (c + 1) : 2], ident[:])
-            hid = ring.tile([P, HALF * PACK], BF16, name="hid", align_bytes=64)
-            dst = hid[:].bitcast(F32).rearrange("p (c e u) -> p c e u", c=2, u=2)
-            src = back[:].rearrange("p c u e -> p c e u")
-            if h == 0:
-                nc.scalar.copy(dst, src)
-            else:
-                nc.vector.tensor_copy(dst, src)
-            hid_codes = ring.tile([P, HALF], U32, name="hid_codes", align_bytes=64)
-            hid_scales = ring.tile([P, HALF], U8, name="hid_scales", align_bytes=64)
+            hid = ring.tile([P, PART * PACK], BF16, name="hid", align_bytes=64)
+            dst = hid[:].bitcast(F32).rearrange("p (c e u) -> p c e u", c=chunks, u=2)
+            nc.scalar.copy(dst, back[:].rearrange("p c u e -> p c e u"))
+            hid_codes = ring.tile([P, PART], U32, name="hid_codes", align_bytes=64)
+            hid_scales = ring.tile([P, PART], U8, name="hid_scales", align_bytes=64)
             nc.vector.quantize_mx(out=hid_codes[:].bitcast(FP8X4), scales=hid_scales[:], in_=hid[:])
-            acc = psum.tile([P, S], F32, name="acc", bufs=2)
+            acc = psum.tile([P, S], F32, name="shade", bufs=2)
             nc.tensor.matmul_mx(
-                out=acc[:, :HALF],
+                out=acc[:, :PART],
                 lhsT=w3_codes[:].bitcast(FP8X4),
                 lhsT_scale=w3_scales[:],
                 rhs=hid_codes[:].bitcast(FP8X4),
@@ -209,12 +251,33 @@ def tile_picked_ymarch_vert_p_kernel(tc, x_words, x_scales, w1, w2, unit, w3, of
                 start=True,
                 stop=True,
             )
-            nc.scalar.copy(shaded[:, h * HALF : (h + 1) * HALF], acc[:, :HALF])
+            nc.vector.tensor_copy(shaded[:, h * PART : (h + 1) * PART], acc[:, :PART])
+
+        features(0)
+        features(1)
+        for t in range(TILES):
+            if t >= 2:
+                magnitudes(t)
+
+        last = TILES - 1
+        nums = []
+        for t in range(TILES + 1):
+            if t < TILES:
+                nums.append(numerators(t, 0, S))
+                squared(t)
+            if t + 2 < TILES:
+                features(t + 2)
+            done = t - 1
+            if 0 <= done < last:
+                edge_factor(done)
+                hidden(done, nums[done], 0, S)
+        for g in range(SPLIT):
+            lo, hi = g * S // SPLIT, (g + 1) * S // SPLIT
+            edge_factor(last, lo, hi)
+            hidden(last, nums[last][:, lo:hi], lo, hi)
+        for h in range(PARTS):
+            shade(h)
         for h in range(2):
             faces = held.tile([P, HALF], F32, name="faces_%d" % h)
-            picked = shaded[:].indirect(fc_sb[:, h * HALF // 16 : (h + 1) * HALF // 16])
-            if h == 0:
-                nc.vector.tensor_copy(faces[:], picked)
-            else:
-                nc.scalar.activation(faces[:], picked, ACT.Copy)
-            nc.sync.dma_start(out[:, h * HALF : (h + 1) * HALF], faces[:])
+            gather(faces[:], shaded, fc_sb[:, h * HALF // 16 : (h + 1) * HALF // 16], h == 0)
+            (nc.sync if h == 0 else nc.scalar).dma_start(out[:, h * HALF : (h + 1) * HALF], faces[:])

@@ -18,13 +18,15 @@ ALU = mybir.AluOpType
 
 P = 128
 PACK = 4
-PASSES = K // (P * PACK)
+K_PASS = P * PACK
+PASSES = K // K_PASS
+QUADRANTS = P // 32
 TILES = H // P
+CHUNKS = S // P
 HALF = S // 2
-PARTS = 4
-PART = S // PARTS
-SPLIT = 2
 WINDOW = 704
+WALK = 4
+EARLY_MAGNITUDES = 2
 
 
 def tile_picked_ymarch_vert_p_kernel(tc, x_words, x_scales, w1, w2, unit, w3, offs, e1, e2, fc, out):
@@ -44,38 +46,40 @@ def tile_picked_ymarch_vert_p_kernel(tc, x_words, x_scales, w1, w2, unit, w3, of
             nc.sync.dma_start(tile[:].bitcast(I32), x_words[o].rearrange("p n j -> p (n j)").bitcast(I32))
             return tile
 
-        def load_weight(name, w, t0, count):
-            raw = held.tile([P, PASSES, PACK, count * P], F32, name="%s_raw_%d" % (name, t0))
+        def weight_rows(w, o, first, count):
+            rows = w[o * K_PASS : (o + 1) * K_PASS, first * P : (first + count) * P]
+            return rows.rearrange("(p j) m -> p j m", j=PACK)
+
+        def load_weight(name, w, first, count):
+            raw = held.tile([P, PASSES, PACK, count * P], F32, name="%s_raw_%d" % (name, first))
             for o in range(PASSES):
-                rows = w[o * P * PACK : (o + 1) * P * PACK, t0 * P : (t0 + count) * P]
-                nc.sync.dma_start(raw[:, o], rows.rearrange("(p j) m -> p j m", j=PACK))
+                nc.sync.dma_start(raw[:, o], weight_rows(w, o, first, count))
             return [raw[:, :, :, i * P : (i + 1) * P] for i in range(count)]
 
-        xs = held.tile([P, T], U8, name="x_scale_rows", tag="scale_rows_then_words", align_bytes=64)
-        nc.gpsimd.memset(xs[:].bitcast(I32), 0)
-        for q in range(4):
-            nc.gpsimd.dma_start(xs[32 * q : 32 * q + 4 * PASSES, :].bitcast(I32), x_scales[:, 4 * q : 4 * q + 4, :].bitcast(I32))
+        scale_rows = held.tile([P, T], U8, name="scale_rows", tag="scale_rows", align_bytes=64)
+        nc.gpsimd.memset(scale_rows[:].bitcast(I32), 0)
+        for q in range(QUADRANTS):
+            nc.scalar.dma_start(
+                scale_rows[32 * q : 32 * q + 4 * PASSES, :].bitcast(I32), x_scales[:, 4 * q : 4 * q + 4, :].bitcast(I32)
+            )
         first_raw = [held.tile([P, PACK, P], F32, name="w2_first_%d" % o) for o in range(PASSES)]
-
-        def load_first(o):
-            nc.sync.dma_start(first_raw[o][:], w2[o * P * PACK : (o + 1) * P * PACK, :P].rearrange("(p j) m -> p j m", j=PACK))
-
-        for o in range(PASSES):
-            load_first(o)
         offs_sb = load_list("offs_sb", offs)
-        xw = [load_words(o) for o in range(PASSES)]
-        raws = [None]
-        lists = (load_list("e1_sb", e1), load_list("e2_sb", e2))
-        raws.extend(load_weight("w2", w2, 1, 1))
-        raws.extend(load_weight("w2", w2, 2, 1))
-        raws.extend(load_weight("w2", w2, 3, 1))
+        edge_lists = (load_list("e1_sb", e1), load_list("e2_sb", e2))
+        for o in range(PASSES):
+            nc.sync.dma_start(first_raw[o][:], weight_rows(w2, o, 0, 1))
+        x_sb = [load_words(o) for o in range(PASSES)]
+        later_raw = []
+        for t in range(1, TILES):
+            later_raw.extend(load_weight("w2", w2, t, 1))
         unit_sb = held.tile([P, TILES], F32, name="unit_sb")
         with nc.allow_non_contiguous_dma(reason="one value of unit a partition and feature tile"):
             nc.sync.dma_start(unit_sb[:], unit.rearrange("(t p) o -> p (t o)", p=P))
-        raws.extend(load_weight("w1", w1, 0, 2))
-        raws.extend(load_weight("w1", w1, 2, 2))
+        for t in range(0, TILES, 2):
+            later_raw.extend(load_weight("w1", w1, t, 2))
         w3_raw = held.tile([P, PACK, N], F32, name="w3_raw")
-        nc.sync.dma_start(w3_raw[:], w3.rearrange("(p j) m -> p j m", j=PACK))
+        w3_rows = w3.rearrange("(g u r e) m -> u g r (e m)", u=2, r=8, e=2)
+        for u in range(2):
+            nc.sync.dma_start(w3_raw[:, 2 * u : 2 * u + 2, :].rearrange("p e m -> p (e m)"), w3_rows[u])
         fc_sb = load_list("fc_sb", fc)
 
         ident = held.tile([P, P], F32, name="ident")
@@ -85,44 +89,43 @@ def tile_picked_ymarch_vert_p_kernel(tc, x_words, x_scales, w1, w2, unit, w3, of
         for tile in signed + feat:
             nc.gpsimd.memset(tile[:, S:], 0.0)
 
-        def quantise_weight(i, grouped, on_scalar=False):
-            dst = grouped[:].rearrange("p (o c i j) -> p o c j i", o=PASSES, i=4, j=PACK)
-            src = raws[i].rearrange("p o j (c i) -> p o c j i", i=4)
-            if on_scalar:
-                nc.scalar.copy(dst, src)
-            else:
-                nc.vector.tensor_copy(dst, src)
+        def quantise_later(i, tag):
+            grouped = held.tile([P, PASSES * P * PACK], BF16, name="grouped_%d" % i, tag=tag, align_bytes=64)
+            nc.vector.tensor_copy(
+                grouped[:].rearrange("p (o c i j) -> p o c j i", o=PASSES, i=WALK, j=PACK),
+                later_raw[i].rearrange("p o j (c i) -> p o c j i", i=WALK),
+            )
             codes = held.tile([P, PASSES * P], U32, name="w_codes_%d" % i, align_bytes=64)
             scales = held.tile([P, PASSES * P], U8, name="w_scales_%d" % i, align_bytes=64)
             nc.vector.quantize_mx(out=codes[:].bitcast(FP8X4), scales=scales[:], in_=grouped[:])
             return codes, scales
 
-        def grouped_tile(i, tag):
-            return held.tile([P, PASSES * P * PACK], BF16, name="grouped_%d" % i, tag=tag, align_bytes=64)
+        def interleave_pass(copy, grouped, raw):
+            copy(grouped[:].rearrange("p (c i j) -> p c j i", i=WALK, j=PACK), raw[:].rearrange("p j (c i) -> p c j i", i=WALK))
 
         def product(weight):
             codes, scales = weight
-            acc = psum.tile([P, S], F32, name="shade", bufs=2)
+            acc = psum.tile([P, S], F32, name="acc", bufs=2)
             for o in range(PASSES):
                 cols = slice(o * P, (o + 1) * P)
                 nc.tensor.matmul_mx(
                     out=acc[:],
                     lhsT=codes[:, cols].bitcast(FP8X4),
                     lhsT_scale=scales[:, cols],
-                    rhs=xg[o][:].bitcast(FP8X4),
-                    rhs_scale=xg_scales[4 * o :, :],
+                    rhs=picked_words[o][:].bitcast(FP8X4),
+                    rhs_scale=picked_scales[4 * o :, :],
                     start=(o == 0),
                     stop=(o == PASSES - 1),
                 )
             return acc
 
-        def turned_sum(tag, bufs, terms, width=S):
+        def turned_sum(tag, bufs, addends):
             bank = psum.tile([P, S], F32, name=tag, bufs=bufs)
-            for c in range(width // P):
+            for c in range(CHUNKS):
                 cols = slice(c * P, (c + 1) * P)
-                for i, term in enumerate(terms):
+                for i, addend in enumerate(addends):
                     nc.tensor.matmul(
-                        bank[:, cols], term[:, cols], ident[:], start=(i == 0), stop=(i == len(terms) - 1), is_transpose=True
+                        bank[:, cols], addend[:, cols], ident[:], start=(i == 0), stop=(i == len(addends) - 1), is_transpose=True
                     )
             return bank
 
@@ -134,116 +137,100 @@ def tile_picked_ymarch_vert_p_kernel(tc, x_words, x_scales, w1, w2, unit, w3, of
 
         first_codes = held.tile([P, PASSES * P], U32, name="first_codes", align_bytes=64)
         first_scales = held.tile([P, PASSES * P], U8, name="first_scales", align_bytes=64)
-
-        def quantise_first(o):
-            grouped = held.tile([P, P * PACK], BF16, name="first_grouped_%d" % o, align_bytes=64)
-            nc.scalar.copy(grouped[:].rearrange("p (c i j) -> p c j i", i=4, j=PACK), first_raw[o][:].rearrange("p j (c i) -> p c j i", i=4))
-            cols = slice(o * P, (o + 1) * P)
-            nc.vector.quantize_mx(out=first_codes[:, cols].bitcast(FP8X4), scales=first_scales[:, cols], in_=grouped[:])
-
         for o in range(PASSES):
-            quantise_first(o)
-        wq = [(first_codes, first_scales)]
-        xg_scales = held.tile([P, S], U8, name="xg_scales", align_bytes=64)
-        xg = [held.tile([P, S], U32, name="xg_words_0", align_bytes=64)]
-        nc.vector.tensor_copy(xg[0][:], xw[0][:].indirect(offs_sb[:]))
-        nc.vector.tensor_copy(xg_scales[:], xs[:].indirect(offs_sb[:]))
-        xg.append(held.tile([P, S], U32, name="xg_words_1", tag="scale_rows_then_words", align_bytes=64))
-        nc.vector.tensor_copy(xg[1][:], xw[1][:].indirect(offs_sb[:]))
-        wq.append(quantise_weight(1, grouped_tile(1, "x_words_1")))
+            first_grouped = held.tile([P, P * PACK], BF16, name="first_grouped_%d" % o, align_bytes=64)
+            interleave_pass(nc.scalar.copy, first_grouped, first_raw[o])
+            cols = slice(o * P, (o + 1) * P)
+            nc.vector.quantize_mx(out=first_codes[:, cols].bitcast(FP8X4), scales=first_scales[:, cols], in_=first_grouped[:])
+        weights = [(first_codes, first_scales)]
+        picked_scales = held.tile([P, S], U8, name="picked_scales", align_bytes=64)
+        picked_words = [held.tile([P, S], U32, name="picked_words_0", align_bytes=64)]
+        nc.vector.tensor_copy(picked_words[0][:], x_sb[0][:].indirect(offs_sb[:]))
+        nc.vector.tensor_copy(picked_scales[:], scale_rows[:].indirect(offs_sb[:]))
+        picked_words.append(held.tile([P, S], U32, name="picked_words_1", tag="scale_rows", align_bytes=64))
+        nc.vector.tensor_copy(picked_words[1][:], x_sb[1][:].indirect(offs_sb[:]))
+        weights.append(quantise_later(0, "x_words_1"))
 
         w3_codes = held.tile([P, N], U32, name="w3_codes", align_bytes=64)
         w3_scales = held.tile([P, N], U8, name="w3_scales", align_bytes=64)
 
-        def quantise_w3():
-            w3_grouped = held.tile([P, N * PACK], BF16, name="w3_grouped", tag="signed_3", align_bytes=64)
-            nc.vector.tensor_copy(
-                w3_grouped[:].rearrange("p (c i j) -> p c j i", i=4, j=PACK), w3_raw[:].rearrange("p j (c i) -> p c j i", i=4)
-            )
-            nc.vector.quantize_mx(out=w3_codes[:].bitcast(FP8X4), scales=w3_scales[:], in_=w3_grouped[:])
-
         ends = [held.tile([P, 2, S], F32, name="ends_%d" % t) for t in range(TILES)]
         mags = [held.tile([P, 2, S], F32, name="mags_%d" % t) for t in range(TILES)]
-        tanh2p = [held.tile([P, S], F32, name="tanh2p_%d" % t) for t in range(TILES)]
+        crossing = [held.tile([P, S], F32, name="crossing_%d" % t) for t in range(TILES)]
         factor = [held.tile([P, S], F32, name="factor_%d" % t) for t in range(TILES)]
-
-        den2 = [held.tile([P, S], F32, name="den2_%d" % t) for t in range(TILES)]
-
-        def squared(t):
-            den = turned_sum("turn_%d" % (t % 2), 1, [mags[t][:, 0, :], mags[t][:, 1, :]])
-            nc.scalar.activation(den2[t][:], den[:], ACT.Square, scale=2.0, bias=0.4)
+        den_sq = [held.tile([P, S], F32, name="den_sq_%d" % t) for t in range(TILES)]
+        last = TILES - 1
 
         def magnitudes(t):
             nc.scalar.activation(mags[t][:], ends[t][:], ACT.Abs)
 
         for t in range(TILES):
-            nc.scalar.activation(signed[t][:, :S], product(wq[t])[:], ACT.Tanh)
+            nc.scalar.activation(signed[t][:, :S], product(weights[t])[:], ACT.Tanh)
             for k in range(2):
-                gather(ends[t][:, k, :], signed[t], lists[k][:], k == 1)
+                gather(ends[t][:, k, :], signed[t], edge_lists[k][:], on_vector=(k == 1))
             prod = ring.tile([P, S], F32, name="prod", tag="prod_%d" % (t % 2), bufs=1)
             nc.vector.tensor_tensor(prod[:], ends[t][:, 0, :], ends[t][:, 1, :], ALU.mult)
-            turned = turned_sum("turn_%d" % (t % 2), 1, [prod])
-            if t < TILES - 1:
-                wq.extend([quantise_weight(i, grouped_tile(i, "signed_%d" % t)) for i in (2 * t + 2, 2 * t + 3)])
+            turned_prod = turned_sum("turn_%d" % (t % 2), 1, [prod])
+            if t < last:
+                weights.extend([quantise_later(i, "signed_%d" % t) for i in (2 * t + 1, 2 * t + 2)])
             else:
-                quantise_w3()
-            if not (t >= 2):
+                w3_grouped = held.tile([P, N * PACK], BF16, name="w3_grouped", tag="signed_%d" % t, align_bytes=64)
+                interleave_pass(nc.vector.tensor_copy, w3_grouped, w3_raw)
+                nc.vector.quantize_mx(out=w3_codes[:].bitcast(FP8X4), scales=w3_scales[:], in_=w3_grouped[:])
+            if t < EARLY_MAGNITUDES:
                 magnitudes(t)
-            nc.scalar.activation(tanh2p[t][:], turned[:], ACT.Tanh, scale=-2.0)
+            nc.scalar.activation(crossing[t][:], turned_prod[:], ACT.Tanh, scale=-2.0)
 
-        rden = ring.tile([P, TILES, S], F32, name="rden", tag="prod_1", bufs=1)
-
-        def edge_factor(t, lo=0, hi=S):
-            nc.scalar.activation(rden[:, t, lo:hi], den2[t][:, lo:hi], ACT.Abs_reciprocal_sqrt)
-            nc.vector.scalar_tensor_tensor(factor[t][:, lo:hi], tanh2p[t][:, lo:hi], 1.0, rden[:, t, lo:hi], ALU.add, ALU.mult)
-
-        hid_t = [held.tile([P, PART // P, H], BF16, name="hid_t_%d" % h) for h in range(PARTS)]
+        inverse = ring.tile([P, TILES, S], F32, name="inverse", tag="prod_%d" % (last % 2), bufs=1)
+        hid_turned = [held.tile([P, H], BF16, name="hid_turned_%d" % c) for c in range(CHUNKS)]
+        shaded = held.tile([P, S], F32, name="shaded")
 
         def features(t):
-            acc = product(wq[TILES + t])
-            if t < 1:
+            acc = product(weights[TILES + t])
+            if t == 0:
                 nc.vector.tensor_scalar(feat[t][:, :S], acc[:], unit_sb[:, t : t + 1], None, ALU.mult)
             else:
                 nc.scalar.activation(feat[t][:, :S], acc[:], ACT.Copy, scale=unit_sb[:, t : t + 1])
 
-        def numerators(t, lo, hi):
-            width = hi - lo
-            terms = []
-            for k in range(2):
-                picked = ring.tile([P, S], F32, name="picked", bufs=4)
-                gather(picked[:, :width], feat[t], lists[k][:, lo // 16 : hi // 16], k == 0)
-                term = ring.tile([P, S], F32, name="term", bufs=4)
-                nc.vector.scalar_tensor_tensor(term[:, :width], mags[t][:, 1 - k, lo:hi], 0.1, picked[:, :width], ALU.add, ALU.mult)
-                terms.append(term)
-            return turned_sum("num", 4, terms, width)
+        def numerator(t):
+            terms = ring.tile([P, 2, S], F32, name="terms")
+            a2 = ring.tile([P, 2, S], F32, name="a2")
+            nc.vector.tensor_scalar(a2[:, 1:, :], mags[t][:, 1:, :], 0.1, None, ALU.add)
+            nc.vector.tensor_tensor(terms[:, 0, :], feat[t][:].indirect(edge_lists[0][:]), a2[:, 1, :], ALU.mult)
+            fb = ring.tile([P, S], F32, name="fb")
+            gather(fb[:], feat[t], edge_lists[1][:], on_vector=False)
+            nc.vector.scalar_tensor_tensor(terms[:, 1, :], mags[t][:, 0, :], 0.1, fb[:], ALU.add, ALU.mult)
+            return turned_sum("num", TILES, [terms[:, 0, :], terms[:, 1, :]])
+
+        def squared_denominator(t):
+            den = turned_sum("turn_%d" % (t % 2), 1, [mags[t][:, 0, :], mags[t][:, 1, :]])
+            nc.scalar.activation(den_sq[t][:], den[:], ACT.Square, scale=2.0, bias=0.4)
 
         def hidden(t, num, lo, hi):
-            for h in range(lo // PART, hi // PART):
+            nc.scalar.activation(inverse[:, t, lo:hi], den_sq[t][:, lo:hi], ACT.Abs_reciprocal_sqrt)
+            nc.vector.scalar_tensor_tensor(factor[t][:, lo:hi], crossing[t][:, lo:hi], 1.0, inverse[:, t, lo:hi], ALU.add, ALU.mult)
+            for c in range(lo // P, hi // P):
+                cols = slice(c * P, (c + 1) * P)
                 nc.vector.tensor_tensor(
-                    hid_t[h][:, :, t * P : (t + 1) * P],
-                    num[:, h * PART - lo : (h + 1) * PART - lo].rearrange("p (c f) -> p c f", f=P),
-                    factor[t][:, h * PART : (h + 1) * PART].rearrange("p (c f) -> p c f", f=P),
+                    hid_turned[c][:].rearrange("p (u t g i) -> p t g u i", u=2, t=TILES, i=16)[:, t],
+                    num[:, cols].rearrange("p (g u i) -> p g u i", u=2, i=16),
+                    factor[t][:, cols].rearrange("p (g u i) -> p g u i", u=2, i=16),
                     ALU.mult,
                 )
 
-        shaded = held.tile([P, S], F32, name="shaded")
-
-        def shade(h):
-            chunks = PART // P
-            words = hid_t[h][:].rearrange("p c f -> p (c f)").bitcast(F32)
-            back = psum.tile([P, chunks, 2, P], F32, name="turn_%d" % (h % 2))
-            for c in range(chunks):
-                for u in range(2):
-                    nc.tensor.transpose(back[:, c, u, :], words[:, 2 * P * c + u : 2 * P * (c + 1) : 2], ident[:])
-            hid = ring.tile([P, PART * PACK], BF16, name="hid", align_bytes=64)
-            dst = hid[:].bitcast(F32).rearrange("p (c e u) -> p c e u", c=chunks, u=2)
-            nc.scalar.copy(dst, back[:].rearrange("p c u e -> p c e u"))
-            hid_codes = ring.tile([P, PART], U32, name="hid_codes", align_bytes=64)
-            hid_scales = ring.tile([P, PART], U8, name="hid_scales", align_bytes=64)
+        def shade(c):
+            words = hid_turned[c][:].bitcast(F32)
+            back = psum.tile([P, 2, P], F32, name="turn_%d" % (c % 2))
+            for u in range(2):
+                nc.tensor.transpose(back[:, u, :], words[:, u * P : (u + 1) * P], ident[:])
+            hid = ring.tile([P, P * PACK], BF16, name="hid", align_bytes=64)
+            nc.scalar.copy(hid[:].bitcast(F32).rearrange("p (e u) -> p e u", u=2), back[:].rearrange("p u e -> p e u"))
+            hid_codes = ring.tile([P, P], U32, name="hid_codes", align_bytes=64)
+            hid_scales = ring.tile([P, P], U8, name="hid_scales", align_bytes=64)
             nc.vector.quantize_mx(out=hid_codes[:].bitcast(FP8X4), scales=hid_scales[:], in_=hid[:])
-            acc = psum.tile([P, S], F32, name="shade", bufs=2)
+            acc = psum.tile([P, S], F32, name="acc", bufs=2)
             nc.tensor.matmul_mx(
-                out=acc[:, :PART],
+                out=acc[:, :P],
                 lhsT=w3_codes[:].bitcast(FP8X4),
                 lhsT_scale=w3_scales[:],
                 rhs=hid_codes[:].bitcast(FP8X4),
@@ -251,33 +238,26 @@ def tile_picked_ymarch_vert_p_kernel(tc, x_words, x_scales, w1, w2, unit, w3, of
                 start=True,
                 stop=True,
             )
-            nc.vector.tensor_copy(shaded[:, h * PART : (h + 1) * PART], acc[:, :PART])
+            nc.vector.tensor_copy(shaded[:, c * P : (c + 1) * P], acc[:, :P])
 
         features(0)
         features(1)
-        for t in range(TILES):
-            if t >= 2:
-                magnitudes(t)
-
-        last = TILES - 1
+        for t in range(EARLY_MAGNITUDES, TILES):
+            magnitudes(t)
         nums = []
-        for t in range(TILES + 1):
-            if t < TILES:
-                nums.append(numerators(t, 0, S))
-                squared(t)
+        for t in range(TILES):
+            nums.append(numerator(t))
+            squared_denominator(t)
             if t + 2 < TILES:
                 features(t + 2)
-            done = t - 1
-            if 0 <= done < last:
-                edge_factor(done)
-                hidden(done, nums[done], 0, S)
-        for g in range(SPLIT):
-            lo, hi = g * S // SPLIT, (g + 1) * S // SPLIT
-            edge_factor(last, lo, hi)
-            hidden(last, nums[last][:, lo:hi], lo, hi)
-        for h in range(PARTS):
-            shade(h)
-        for h in range(2):
+            if t > 0:
+                hidden(t - 1, nums[t - 1], 0, S)
+        for lo in range(0, S, HALF):
+            hidden(last, nums[last], lo, lo + HALF)
+        for c in range(CHUNKS):
+            shade(c)
+
+        for h, queue in enumerate((nc.sync, nc.scalar)):
             faces = held.tile([P, HALF], F32, name="faces_%d" % h)
-            gather(faces[:], shaded, fc_sb[:, h * HALF // 16 : (h + 1) * HALF // 16], h == 0)
-            (nc.sync if h == 0 else nc.scalar).dma_start(out[:, h * HALF : (h + 1) * HALF], faces[:])
+            gather(faces[:], shaded, fc_sb[:, h * HALF // 16 : (h + 1) * HALF // 16], on_vector=(h == 0))
+            queue.dma_start(out[:, h * HALF : (h + 1) * HALF], faces[:])

from contextlib import ExitStack

import concourse.mybir as mybir
from concourse.masks import make_identity

K, T, S, N, H = 1024, 2048, 512, 128, 512
FLOPS = 2 * (2 * K * H * S + H * N * S)

F32 = mybir.dt.float32
BF16 = mybir.dt.bfloat16
I32 = mybir.dt.int32
U32 = mybir.dt.uint32
U16 = mybir.dt.uint16
U8 = mybir.dt.uint8
FP8X4 = mybir.dt.float8_e4m3fn_x4
ACT = mybir.ActivationFunctionType
ALU = mybir.AluOpType

P = 128
PACK = 4
K_PASS = P * PACK
PASSES = K // K_PASS
QUADRANTS = P // 32
TILES = H // P
CHUNKS = S // P
HALF = S // 2
WINDOW = 704
WALK = 4
EARLY_MAGNITUDES = 2


def tile_picked_ymarch_vert_p_kernel(tc, x_words, x_scales, w1, w2, unit, w3, offs, e1, e2, fc, out):
    nc = tc.nc
    with ExitStack() as ctx:
        held = ctx.enter_context(tc.tile_pool(name="held", bufs=1))
        ring = ctx.enter_context(tc.tile_pool(name="ring", bufs=2))
        psum = ctx.enter_context(tc.psum_pool(name="psum", bufs=1))

        def load_list(name, dram):
            tile = held.tile([P, S // 16], U16, name=name)
            nc.sync.dma_start(tile[:], dram)
            return tile

        def load_words(o):
            tile = held.tile([P, T], U32, name="x_words_%d" % o, tag="x_words_%d" % o, align_bytes=64)
            nc.sync.dma_start(tile[:].bitcast(I32), x_words[o].rearrange("p n j -> p (n j)").bitcast(I32))
            return tile

        def weight_rows(w, o, first, count):
            rows = w[o * K_PASS : (o + 1) * K_PASS, first * P : (first + count) * P]
            return rows.rearrange("(p j) m -> p j m", j=PACK)

        def load_weight(name, w, first, count):
            raw = held.tile([P, PASSES, PACK, count * P], F32, name="%s_raw_%d" % (name, first))
            for o in range(PASSES):
                nc.sync.dma_start(raw[:, o], weight_rows(w, o, first, count))
            return [raw[:, :, :, i * P : (i + 1) * P] for i in range(count)]

        scale_rows = held.tile([P, T], U8, name="scale_rows", tag="scale_rows", align_bytes=64)
        nc.gpsimd.memset(scale_rows[:].bitcast(I32), 0)
        for q in range(QUADRANTS):
            nc.scalar.dma_start(
                scale_rows[32 * q : 32 * q + 4 * PASSES, :].bitcast(I32), x_scales[:, 4 * q : 4 * q + 4, :].bitcast(I32)
            )
        first_raw = [held.tile([P, PACK, P], F32, name="w2_first_%d" % o) for o in range(PASSES)]
        offs_sb = load_list("offs_sb", offs)
        edge_lists = (load_list("e1_sb", e1), load_list("e2_sb", e2))
        for o in range(PASSES):
            nc.sync.dma_start(first_raw[o][:], weight_rows(w2, o, 0, 1))
        x_sb = [load_words(o) for o in range(PASSES)]
        later_raw = []
        for t in range(1, TILES):
            later_raw.extend(load_weight("w2", w2, t, 1))
        unit_sb = held.tile([P, TILES], F32, name="unit_sb")
        with nc.allow_non_contiguous_dma(reason="one value of unit a partition and feature tile"):
            nc.sync.dma_start(unit_sb[:], unit.rearrange("(t p) o -> p (t o)", p=P))
        for t in range(0, TILES, 2):
            later_raw.extend(load_weight("w1", w1, t, 2))
        w3_raw = held.tile([P, PACK, N], F32, name="w3_raw")
        w3_rows = w3.rearrange("(g u r e) m -> u g r (e m)", u=2, r=8, e=2)
        for u in range(2):
            nc.sync.dma_start(w3_raw[:, 2 * u : 2 * u + 2, :].rearrange("p e m -> p (e m)"), w3_rows[u])
        fc_sb = load_list("fc_sb", fc)

        ident = held.tile([P, P], F32, name="ident")
        make_identity(nc, ident[:])
        signed = [held.tile([P, WINDOW], F32, name="signed_%d" % t, tag="signed_%d" % t, align_bytes=64) for t in range(TILES)]
        feat = [held.tile([P, WINDOW], F32, name="feat_%d" % t) for t in range(TILES)]
        for tile in signed + feat:
            nc.gpsimd.memset(tile[:, S:], 0.0)

        def quantise_later(i, tag):
            grouped = held.tile([P, PASSES * P * PACK], BF16, name="grouped_%d" % i, tag=tag, align_bytes=64)
            nc.vector.tensor_copy(
                grouped[:].rearrange("p (o c i j) -> p o c j i", o=PASSES, i=WALK, j=PACK),
                later_raw[i].rearrange("p o j (c i) -> p o c j i", i=WALK),
            )
            codes = held.tile([P, PASSES * P], U32, name="w_codes_%d" % i, align_bytes=64)
            scales = held.tile([P, PASSES * P], U8, name="w_scales_%d" % i, align_bytes=64)
            nc.vector.quantize_mx(out=codes[:].bitcast(FP8X4), scales=scales[:], in_=grouped[:])
            return codes, scales

        def interleave_pass(copy, grouped, raw):
            copy(grouped[:].rearrange("p (c i j) -> p c j i", i=WALK, j=PACK), raw[:].rearrange("p j (c i) -> p c j i", i=WALK))

        def product(weight):
            codes, scales = weight
            acc = psum.tile([P, S], F32, name="acc", bufs=2)
            for o in range(PASSES):
                cols = slice(o * P, (o + 1) * P)
                nc.tensor.matmul_mx(
                    out=acc[:],
                    lhsT=codes[:, cols].bitcast(FP8X4),
                    lhsT_scale=scales[:, cols],
                    rhs=picked_words[o][:].bitcast(FP8X4),
                    rhs_scale=picked_scales[4 * o :, :],
                    start=(o == 0),
                    stop=(o == PASSES - 1),
                )
            return acc

        def turned_sum(tag, bufs, addends):
            bank = psum.tile([P, S], F32, name=tag, bufs=bufs)
            for c in range(CHUNKS):
                cols = slice(c * P, (c + 1) * P)
                for i, addend in enumerate(addends):
                    nc.tensor.matmul(
                        bank[:, cols], addend[:, cols], ident[:], start=(i == 0), stop=(i == len(addends) - 1), is_transpose=True
                    )
            return bank

        def gather(dst, window, offsets, on_vector):
            if on_vector:
                nc.vector.tensor_copy(dst, window[:].indirect(offsets))
            else:
                nc.scalar.activation(dst, window[:].indirect(offsets), ACT.Copy)

        first_codes = held.tile([P, PASSES * P], U32, name="first_codes", align_bytes=64)
        first_scales = held.tile([P, PASSES * P], U8, name="first_scales", align_bytes=64)
        for o in range(PASSES):
            first_grouped = held.tile([P, P * PACK], BF16, name="first_grouped_%d" % o, align_bytes=64)
            interleave_pass(nc.scalar.copy, first_grouped, first_raw[o])
            cols = slice(o * P, (o + 1) * P)
            nc.vector.quantize_mx(out=first_codes[:, cols].bitcast(FP8X4), scales=first_scales[:, cols], in_=first_grouped[:])
        weights = [(first_codes, first_scales)]
        picked_scales = held.tile([P, S], U8, name="picked_scales", align_bytes=64)
        picked_words = [held.tile([P, S], U32, name="picked_words_0", align_bytes=64)]
        nc.vector.tensor_copy(picked_words[0][:], x_sb[0][:].indirect(offs_sb[:]))
        nc.vector.tensor_copy(picked_scales[:], scale_rows[:].indirect(offs_sb[:]))
        picked_words.append(held.tile([P, S], U32, name="picked_words_1", tag="scale_rows", align_bytes=64))
        nc.vector.tensor_copy(picked_words[1][:], x_sb[1][:].indirect(offs_sb[:]))
        weights.append(quantise_later(0, "x_words_1"))

        w3_codes = held.tile([P, N], U32, name="w3_codes", align_bytes=64)
        w3_scales = held.tile([P, N], U8, name="w3_scales", align_bytes=64)

        ends = [held.tile([P, 2, S], F32, name="ends_%d" % t) for t in range(TILES)]
        mags = [held.tile([P, 2, S], F32, name="mags_%d" % t) for t in range(TILES)]
        crossing = [held.tile([P, S], F32, name="crossing_%d" % t) for t in range(TILES)]
        factor = [held.tile([P, S], F32, name="factor_%d" % t) for t in range(TILES)]
        den_sq = [held.tile([P, S], F32, name="den_sq_%d" % t) for t in range(TILES)]
        last = TILES - 1

        def magnitudes(t):
            nc.scalar.activation(mags[t][:], ends[t][:], ACT.Abs)

        for t in range(TILES):
            nc.scalar.activation(signed[t][:, :S], product(weights[t])[:], ACT.Tanh)
            for k in range(2):
                gather(ends[t][:, k, :], signed[t], edge_lists[k][:], on_vector=(k == 1))
            prod = ring.tile([P, S], F32, name="prod", tag="prod_%d" % (t % 2), bufs=1)
            nc.vector.tensor_tensor(prod[:], ends[t][:, 0, :], ends[t][:, 1, :], ALU.mult)
            turned_prod = turned_sum("turn_%d" % (t % 2), 1, [prod])
            if t < last:
                weights.extend([quantise_later(i, "signed_%d" % t) for i in (2 * t + 1, 2 * t + 2)])
            else:
                w3_grouped = held.tile([P, N * PACK], BF16, name="w3_grouped", tag="signed_%d" % t, align_bytes=64)
                interleave_pass(nc.vector.tensor_copy, w3_grouped, w3_raw)
                nc.vector.quantize_mx(out=w3_codes[:].bitcast(FP8X4), scales=w3_scales[:], in_=w3_grouped[:])
            if t < EARLY_MAGNITUDES:
                magnitudes(t)
            nc.scalar.activation(crossing[t][:], turned_prod[:], ACT.Tanh, scale=-2.0)

        inverse = ring.tile([P, TILES, S], F32, name="inverse", tag="prod_%d" % (last % 2), bufs=1)
        hid_turned = [held.tile([P, H], BF16, name="hid_turned_%d" % c) for c in range(CHUNKS)]
        shaded = held.tile([P, S], F32, name="shaded")

        def features(t):
            acc = product(weights[TILES + t])
            if t == 0:
                nc.vector.tensor_scalar(feat[t][:, :S], acc[:], unit_sb[:, t : t + 1], None, ALU.mult)
            else:
                nc.scalar.activation(feat[t][:, :S], acc[:], ACT.Copy, scale=unit_sb[:, t : t + 1])

        def numerator(t):
            terms = ring.tile([P, 2, S], F32, name="terms")
            a2 = ring.tile([P, 2, S], F32, name="a2")
            nc.vector.tensor_scalar(a2[:, 1:, :], mags[t][:, 1:, :], 0.1, None, ALU.add)
            nc.vector.tensor_tensor(terms[:, 0, :], feat[t][:].indirect(edge_lists[0][:]), a2[:, 1, :], ALU.mult)
            fb = ring.tile([P, S], F32, name="fb")
            gather(fb[:], feat[t], edge_lists[1][:], on_vector=False)
            nc.vector.scalar_tensor_tensor(terms[:, 1, :], mags[t][:, 0, :], 0.1, fb[:], ALU.add, ALU.mult)
            return turned_sum("num", TILES, [terms[:, 0, :], terms[:, 1, :]])

        def squared_denominator(t):
            den = turned_sum("turn_%d" % (t % 2), 1, [mags[t][:, 0, :], mags[t][:, 1, :]])
            nc.scalar.activation(den_sq[t][:], den[:], ACT.Square, scale=2.0, bias=0.4)

        def hidden(t, num, lo, hi):
            nc.scalar.activation(inverse[:, t, lo:hi], den_sq[t][:, lo:hi], ACT.Abs_reciprocal_sqrt)
            nc.vector.scalar_tensor_tensor(factor[t][:, lo:hi], crossing[t][:, lo:hi], 1.0, inverse[:, t, lo:hi], ALU.add, ALU.mult)
            for c in range(lo // P, hi // P):
                cols = slice(c * P, (c + 1) * P)
                nc.vector.tensor_tensor(
                    hid_turned[c][:].rearrange("p (u t g i) -> p t g u i", u=2, t=TILES, i=16)[:, t],
                    num[:, cols].rearrange("p (g u i) -> p g u i", u=2, i=16),
                    factor[t][:, cols].rearrange("p (g u i) -> p g u i", u=2, i=16),
                    ALU.mult,
                )

        def shade(c):
            words = hid_turned[c][:].bitcast(F32)
            back = psum.tile([P, 2, P], F32, name="turn_%d" % (c % 2))
            for u in range(2):
                nc.tensor.transpose(back[:, u, :], words[:, u * P : (u + 1) * P], ident[:])
            hid = ring.tile([P, P * PACK], BF16, name="hid", align_bytes=64)
            nc.scalar.copy(hid[:].bitcast(F32).rearrange("p (e u) -> p e u", u=2), back[:].rearrange("p u e -> p e u"))
            hid_codes = ring.tile([P, P], U32, name="hid_codes", align_bytes=64)
            hid_scales = ring.tile([P, P], U8, name="hid_scales", align_bytes=64)
            nc.vector.quantize_mx(out=hid_codes[:].bitcast(FP8X4), scales=hid_scales[:], in_=hid[:])
            acc = psum.tile([P, S], F32, name="acc", bufs=2)
            nc.tensor.matmul_mx(
                out=acc[:, :P],
                lhsT=w3_codes[:].bitcast(FP8X4),
                lhsT_scale=w3_scales[:],
                rhs=hid_codes[:].bitcast(FP8X4),
                rhs_scale=hid_scales[:],
                start=True,
                stop=True,
            )
            nc.vector.tensor_copy(shaded[:, c * P : (c + 1) * P], acc[:, :P])

        features(0)
        features(1)
        for t in range(EARLY_MAGNITUDES, TILES):
            magnitudes(t)
        nums = []
        for t in range(TILES):
            nums.append(numerator(t))
            squared_denominator(t)
            if t + 2 < TILES:
                features(t + 2)
            if t > 0:
                hidden(t - 1, nums[t - 1], 0, S)
        for lo in range(0, S, HALF):
            hidden(last, nums[last], lo, lo + HALF)
        for c in range(CHUNKS):
            shade(c)

        for h, queue in enumerate((nc.sync, nc.scalar)):
            faces = held.tile([P, HALF], F32, name="faces_%d" % h)
            gather(faces[:], shaded, fc_sb[:, h * HALF // 16 : (h + 1) * HALF // 16], on_vector=(h == 0))
            queue.dma_start(out[:, h * HALF : (h + 1) * HALF], faces[:])
